import numpy as np, ml_dtypes
CORES = [0,1,2,3,4,5,6,7]
N = 8
PERM = [[0,1],[1,7],[2,5],[3,6],[4,3],[5,0],[6,4],[7,2]]
def setup_inputs(rng):
    return {"x": rng.standard_normal((N, 128, 2), dtype=np.float32).astype(ml_dtypes.bfloat16)}
def reference(x):
    y = np.empty_like(x)
    for s, d in PERM:
        y[d] = x[s]
    return {"y": y}

SCRATCH = {
    "stage": ("dram", [128, 2], "bfloat16"),
    "land": ("dram", [128, 2], "bfloat16"),
}
SEMAPHORES = ["loaded", "sent", "arrived", "stored"]

ENGINE_MASK = 0x0001
ENGINES = 1


def rank_program(g, core, T, topo):
    rank = T.rank_of(core)
    if rank is None:
        return

    dst_of = {s: d for s, d in T.tables["PERM"]}
    src_of = {d: s for s, d in T.tables["PERM"]}
    dst = dst_of.get(rank)
    src = src_of.get(rank)

    if src == rank:
        g.sync.dma_start(T.y[:], T.x[:]).then_inc(T.sem.stored, 16)
        g.sync.wait_ge(T.sem.stored, 16)
        return

    if dst is not None:
        g.sync.dma_start(T.stage[:], T.x[:]).then_inc(T.sem.loaded, 16)
        g.wait_ge(T.sem.loaded, 16)
        rid, pid, _se = topo.addr(T.cores[dst])
        g.remote_dma(
            T.land[:], T.stage[:],
            remote_sem=T.sem.arrived, local_sem=T.sem.sent,
            pid=pid, routing_id=rid, dma_engine_mask=ENGINE_MASK,
        )

    if src is not None:
        g.sync.wait_ge(T.sem.arrived, ENGINES)
        g.sync.dma_start(T.y[:], T.land[:]).then_inc(T.sem.stored, 16)
        g.sync.wait_ge(T.sem.stored, 16)

    if dst is not None:
        g.wait_ge(T.sem.sent, ENGINES)
